import numpy as np
import ml_dtypes


def mxq(x, axis, fmt="e4m3"):
    dtype, down = {"e4m3": (ml_dtypes.float8_e4m3fn, 7), "e5m2": (ml_dtypes.float8_e5m2, 14)}[fmt]
    v = np.moveaxis(np.asarray(x, np.float32).astype(ml_dtypes.bfloat16).astype(np.float64), axis, -1)
    blocks = v.reshape(v.shape[:-1] + (-1, 32))
    amax = np.abs(blocks).max(-1, keepdims=True)
    byte = np.maximum(np.where(amax > 0, np.frexp(amax)[1] - 1 + 127, 0) - down, 1)
    scale = np.exp2(byte - 127.0)
    codes = (blocks / scale).astype(np.float32).astype(dtype).astype(np.float64)
    return np.moveaxis((codes * scale).reshape(v.shape), -1, axis)


WIDE = False


def mx_kscale(k):
    if not WIDE:
        return np.ones(k)
    levels = np.array([10, -10, 5, -5, 0])
    if k % 512:
        return np.exp2(np.random.permutation(np.resize(levels, k // 32))).repeat(32)
    a = np.empty((k // 512, 16))
    for p in range(k // 512):
        a[p, :8] = np.random.permutation(np.resize(levels, 8))
        for g in range(8):
            far = levels[np.abs(levels - a[p, g]) >= 10]
            a[p, g + 8] = far[np.random.randint(len(far))]
    return np.exp2(a.ravel()).repeat(32)


def f64(x):
    return np.asarray(x).astype(np.float64)


def striped(idx):
    return np.tile(np.asarray(idx).reshape(-1, 16).T, (8, 1)).astype(np.uint16)


def unstriped(offs):
    return offs[:16].T.reshape(-1).astype(np.int64)


def striped8(idx):
    return np.asarray(idx).reshape(8, -1, 16).transpose(0, 2, 1).reshape(128, -1).astype(np.uint16)


def unstriped8(offs):
    return offs.reshape(8, 16, -1).transpose(0, 2, 1).reshape(8, -1).astype(np.int64)


def pick8(x, idx, run):
    r = np.arange(len(x))
    return x[r[:, None], idx[r % (8 * run) // run]]


E2M1 = np.array([0.0, 0.5, 1.0, 1.5, 2.0, 3.0, 4.0, 6.0, -0.0, -0.5, -1.0, -1.5, -2.0, -3.0, -4.0, -6.0])


def pack_weight(w, fmt):
    k, n = w.shape
    w = f64(np.asarray(w, np.float32).astype(ml_dtypes.bfloat16)).reshape(k // 32, 32, n)
    amax = np.abs(w).max(1)
    if fmt == "e4m3":
        byte = np.frexp(amax)[1] - 1 + 127 - 7
    else:
        mant, ex = np.frexp(amax / 6.0)
        byte = np.where(mant > 0.5, ex, ex - 1) + 127
    byte = np.clip(np.where(amax > 0, byte, 1), 1, 254)
    scaled = (w * np.exp2(127.0 - byte)[:, None, :]).reshape(k, n).astype(np.float32)
    by_word = np.ascontiguousarray(scaled.reshape(k // 512, 128, 4, n).transpose(0, 1, 3, 2))
    if fmt == "e4m3":
        words = by_word.astype(ml_dtypes.float8_e4m3fn).view(np.uint8)
    else:
        c = by_word.astype(ml_dtypes.float4_e2m1fn).view(np.uint8) & 0xF
        words = (c[..., 0::2] | (c[..., 1::2] << 4)).reshape(k // 512, 128, 2 * n)
    return np.ascontiguousarray(words), np.ascontiguousarray(byte.astype(np.uint8).reshape(k // 512, 16, n))


def unpack_weight(words, scales, fmt):
    g, _, n = scales.shape
    words = np.ascontiguousarray(words).reshape(g, 128, n, -1)
    if fmt == "e4m3":
        vals = words.view(ml_dtypes.float8_e4m3fn).astype(np.float64)
    else:
        nib = np.empty((g, 128, n, 4), np.uint8)
        nib[..., 0::2] = words & 0xF
        nib[..., 1::2] = words >> 4
        vals = E2M1[nib]
    vals = vals * np.repeat(np.exp2(scales.astype(np.float64) - 127.0), 8, axis=1)[..., None]
    return vals.transpose(0, 1, 3, 2).reshape(g * 512, n)


K, J, R, T, Z, M, S, U, C, O, N, V = 512, 512, 512, 2048, 512, 1024, 256, 128, 256, 128, 256, 1024


def setup_inputs():
    n = np.random.standard_normal
    idx = np.random.permutation(T)[:J]
    idx2 = np.random.permutation(M)[:J]
    idx3 = np.stack([np.random.permutation(J)[:S] for _ in range(8)])
    idx4 = np.stack([np.random.permutation(C)[:U] for _ in range(8)])
    idx5 = np.stack([np.random.permutation(C)[:O] for _ in range(8)])
    idx6 = np.random.permutation(V)[:N]
    fk = mx_kscale(K)
    fr = mx_kscale(R)
    fz = mx_kscale(Z)
    xtp = pack_weight(n((K, T)) * fk[:, None], "e2m1")
    wp = pack_weight(n((K, R)) * 1 / np.sqrt(K) / fk[:, None] * fr, "e4m3")
    xop = pack_weight(n((Z, M)) / fz[:, None], "e4m3")
    w2p = pack_weight(n((Z, R)) * 1 / np.sqrt(Z) * fz[:, None] * fr, "e2m1")
    vsp = pack_weight(n((R, V)) * 1 / np.sqrt(R) / fr[:, None], "e2m1")
    return {
        "xt_words": xtp[0],
        "xt_scales": xtp[1],
        "w_words": wp[0],
        "w_scales": wp[1],
        "xo_words": xop[0],
        "xo_scales": xop[1],
        "w2_words": w2p[0],
        "w2_scales": w2p[1],
        "sa": (np.random.uniform(0.5, 1.6, (R, 1))).astype(np.float32),
        "sb": (np.random.uniform(0.5, 1.6, (R, 1))).astype(np.float32),
        "vs_words": vsp[0],
        "vs_scales": vsp[1],
        "offs": striped(idx),
        "offs2": striped(idx2),
        "offs3": striped8(idx3),
        "offs4": striped8(idx4),
        "offs5": striped8(idx5),
        "offs6": striped(idx6),
    }


def reference(xt_words, xt_scales, w_words, w_scales, xo_words, xo_scales, w2_words, w2_scales, sa, sb, vs_words, vs_scales, offs, offs2, offs3, offs4, offs5, offs6):
    idx = unstriped(offs)
    idx2 = unstriped(offs2)
    idx3 = unstriped8(offs3)
    idx4 = unstriped8(offs4)
    idx5 = unstriped8(offs5)
    idx6 = unstriped(offs6)
    xtu = unpack_weight(xt_words, xt_scales, "e2m1")
    wu = unpack_weight(w_words, w_scales, "e4m3")
    xou = unpack_weight(xo_words, xo_scales, "e4m3")
    w2u = unpack_weight(w2_words, w2_scales, "e2m1")
    vsu = unpack_weight(vs_words, vs_scales, "e2m1")
    xtidxg = xtu[:, idx]
    xoidx2g = xou[:, idx2]
    a = wu.T @ xtidxg + w2u.T @ xoidx2g
    h1 = pick8(a, idx3, 64) * f64(sa)
    h2 = h1.reshape(R, U, S // U).max(axis=2)
    pw = np.zeros((R, C))
    pw[np.arange(R)[:, None], idx4[np.arange(R) % 512 // 64]] = h2
    hid = pick8(pw, idx5, 64) * f64(sb)
    vsidx6g = vsu[:, idx6]
    hidq = mxq(hid, 0, "e4m3")
    y = vsidx6g.T @ hidq
    return y

@@ -1,0 +1,190 @@
+from contextlib import ExitStack
+
+import concourse.mybir as mybir
+
+F32 = mybir.dt.float32
+BF16 = mybir.dt.bfloat16
+I32 = mybir.dt.int32
+U32 = mybir.dt.uint32
+U16 = mybir.dt.uint16
+U8 = mybir.dt.uint8
+FP8X4 = mybir.dt.float8_e4m3fn_x4
+FP4X4 = mybir.dt.float4_e2m1fn_x4
+COPY = mybir.ActivationFunctionType.Copy
+MAX = mybir.AluOpType.max
+
+K, J, R, T, Z, M, S, U, C, O, N, V = 512, 512, 512, 2048, 512, 1024, 256, 128, 256, 128, 256, 1024
+FLOPS = 2 * K * R * J + 2 * Z * R * J + 2 * R * N * O
+
+P = 128
+PACK = 4
+HALF = J // 2
+
+
+def tile_picked_tokens_plain_bank_pooledpost_store_plain_kernel(
+    tc, xt_words, xt_scales, w_words, w_scales, xo_words, xo_scales, w2_words, w2_scales,
+    sa, sb, vs_words, vs_scales, offs, offs2, offs3, offs4, offs5, offs6, out,
+):
+    nc = tc.nc
+    with ExitStack() as ctx:
+        keep = ctx.enter_context(tc.tile_pool(name="keep", bufs=1))
+        psum = ctx.enter_context(tc.psum_pool(name="psum", bufs=1))
+
+        def sbuf(shape, dtype, name):
+            return keep.tile(shape, dtype, name=name, align_bytes=64)
+
+        def load_list(src, name):
+            tile = keep.tile(list(src.shape), U16, name=name)
+            nc.sync.dma_start(tile[:], src)
+            return tile
+
+        def zeroed_plane(width, name):
+            tile = sbuf([P, width], U8, name)
+            nc.vector.memset(tile[:].bitcast(I32), 0)
+            return tile
+
+        def load_plane(queue, tile, src, quadrants=range(4)):
+            for q in quadrants:
+                queue.dma_start(tile[32 * q : 32 * q + 4, :].bitcast(I32), src[0, 4 * q : 4 * q + 4, :].bitcast(I32))
+
+        def load_words(queue, dtype, width, src, name):
+            tile = sbuf([P, width], dtype, name)
+            queue.dma_start(tile[:].bitcast(I32), src.bitcast(I32))
+            return tile
+
+        xo_s = zeroed_plane(M, "xo_s")
+        xt_s = zeroed_plane(T, "xt_s")
+        w2_s = zeroed_plane(R, "w2_s")
+        w_s = zeroed_plane(R, "w_s")
+        vs_s = zeroed_plane(V, "vs_s")
+        boards = [sbuf([P, C], F32, f"board{t}") for t in range(PACK)]
+        for t in range(PACK):
+            nc.vector.memset(boards[t][:], 0.0)
+
+        l2 = load_list(offs2, "l2")
+        l1 = load_list(offs, "l1")
+        l3 = load_list(offs3, "l3")
+        load_plane(nc.sync, xo_s, xo_scales)
+        xo_w = load_words(nc.sync, U32, M, xo_words[0].rearrange("p n t -> p (n t)"), "xo_w")
+        xt_w = load_words(nc.sync, U16, T, xt_words[0], "xt_w")
+        load_plane(nc.sync, xt_s, xt_scales)
+        w2_w = load_words(nc.sync, U16, R, w2_words[0], "w2_w")
+        w_w = load_words(nc.sync, U32, R, w_words[0].rearrange("p n t -> p (n t)"), "w_w")
+        load_plane(nc.sync, w2_s, w2_scales, range(0, 4))
+        load_plane(nc.sync, w_s, w_scales)
+        sa_t = sbuf([P, PACK], F32, "sa_t")
+        nc.sync.dma_start(sa_t[:], sa.rearrange("(p t) o -> p (t o)", t=PACK))
+        l4 = load_list(offs4, "l4")
+        l5 = load_list(offs5, "l5")
+        sb_t = sbuf([P, PACK], F32, "sb_t")
+        nc.sync.dma_start(sb_t[:], sb.rearrange("(p t) o -> p (t o)", t=PACK))
+        l6 = load_list(offs6, "l6")
+        vs_w = load_words(nc.sync, U16, V, vs_words[0], "vs_w")
+        load_plane(nc.sync, vs_s, vs_scales)
+
+        def deal(copy, src, dtype, name):
+            tile = sbuf([P, R], dtype, name)
+            copy(tile[:].rearrange("p (t m) -> p m t", t=PACK), src[:].rearrange("p (m t) -> p m t", t=PACK))
+            return tile
+
+        def gather(src, offsets, count, dtype, name):
+            tile = sbuf([P, count], dtype, name)
+            nc.vector.tensor_copy(tile[:], src[:].indirect(offsets))
+            return tile
+
+        w2_wd = deal(nc.scalar.copy, w2_w, U16, "w2_wd")
+        w_wd = deal(nc.scalar.copy, w_w, U32, "w_wd")
+
+        xo_sg = gather(xo_s, l2[:], J, U8, "xo_sg")
+        xo_wg = gather(xo_w, l2[:], J, U32, "xo_wg")
+        w2_sd = deal(nc.vector.tensor_copy, w2_s, U8, "w2_sd")
+        w_sd = deal(nc.vector.tensor_copy, w_s, U8, "w_sd")
+        halves = [l1[:, h * HALF // 16 : (h + 1) * HALF // 16] for h in range(2)]
+        xt_wg = [gather(xt_w, halves[0], HALF, U16, "xt_wg0")]
+        xt_sg = [gather(xt_s, halves[0], HALF, U8, "xt_sg0")]
+        xt_wg.append(gather(xt_w, halves[1], HALF, U16, "w2_s"))
+        xt_sg.append(gather(xt_s, halves[1], HALF, U8, "w_s"))
+
+        def product(acc, t, h, notes_first):
+            rows = slice(t * P, (t + 1) * P)
+            cols = slice(h * HALF, (h + 1) * HALF)
+            notes = dict(
+                lhsT=w2_wd[:, rows].bitcast(FP4X4), lhsT_scale=w2_sd[:, rows],
+                rhs=xo_wg[:, cols].bitcast(FP8X4), rhs_scale=xo_sg[:, cols],
+            )
+            tokens = dict(
+                lhsT=w_wd[:, rows].bitcast(FP8X4), lhsT_scale=w_sd[:, rows],
+                rhs=xt_wg[h][:].bitcast(FP4X4), rhs_scale=xt_sg[h][:],
+            )
+            opening, closing = (notes, tokens) if notes_first else (tokens, notes)
+            nc.tensor.matmul_mx(acc, start=True, stop=False, **opening)
+            nc.tensor.matmul_mx(acc, start=False, stop=True, **closing)
+
+        a, picks, pooled = {}, {}, {}
+        woven = sbuf([P, O, PACK], BF16, "woven")
+
+        def finish_a(t):
+            if t < 2:
+                a[t] = sbuf([P, J], F32, f"a{t}")
+                first = psum.tile([P, HALF], F32, name=f"first{t}")
+                second = psum.tile([P, HALF], F32, name=f"second{t}")
+                product(first[:], t, 0, True)
+                product(second[:], t, 1, True)
+                nc.scalar.copy(a[t][:, :HALF], first[:])
+                nc.vector.tensor_copy(a[t][:, HALF:], second[:])
+            else:
+                a[t] = sbuf([P, J], F32, f"picks{t - 2}")
+                both = psum.tile([P, J], F32, name=f"both{t}")
+                product(both[:, HALF:], t, 1, False)
+                product(both[:, :HALF], t, 0, False)
+                nc.vector.tensor_copy(a[t][:], both[:])
+
+        def pick(t):
+            picks[t] = sbuf([P, S], F32, f"picks{t}")
+            nc.scalar.activation(picks[t][:], a[t][:].indirect(l3[:]), COPY, scale=sa_t[:, t : t + 1])
+
+        def pool_pairs(t):
+            pooled[t] = sbuf([P, U], F32, f"pooled{t}")
+            nc.vector.tensor_tensor(pooled[t][:], picks[t][:, 0:S:2], picks[t][:, 1:S:2], MAX)
+
+        def put(t):
+            nc.scalar.activation(boards[t][:].indirect(l4[:]), pooled[t][:], COPY)
+
+        finish_a(0)
+        finish_a(1)
+        pick(0)
+        for t in range(PACK):
+            pool_pairs(t)
+            if t + 2 < PACK:
+                finish_a(t + 2)
+            if t + 1 < PACK:
+                pick(t + 1)
+            put(t)
+
+        vs_sg = gather(vs_s, l6[:], N, U8, "picks2")
+        vs_wg = gather(vs_w, l6[:], N, U16, "picks1")
+
+        hid = sbuf([P, PACK, O], BF16, "picks3")
+        for t in range(PACK):
+            nc.scalar.activation(hid[:, t, :], boards[t][:].indirect(l5[:]), COPY, scale=sb_t[:, t : t + 1])
+        nc.vector.tensor_copy(woven[:, :, 0:2], hid[:, 0:2, :].rearrange("p t o -> p o t"))
+        nc.vector.tensor_copy(woven[:, :, 2], hid[:, 2, :])
+        nc.vector.tensor_copy(woven[:, :, 3], hid[:, 3, :])
+        hid_w = sbuf([P, O], U32, "hid_w")
+        hid_s = sbuf([P, O], U8, "hid_s")
+        nc.vector.quantize_mx(out=hid_w[:].bitcast(FP8X4), scales=hid_s[:], in_=woven[:].rearrange("p o t -> p (o t)"))
+
+        for b in range(N // P):
+            rows = slice(b * P, (b + 1) * P)
+            acc = psum.tile([P, O], F32, name=f"acc{b}")
+            nc.tensor.matmul_mx(
+                acc[:], lhsT=vs_wg[:, rows].bitcast(FP4X4), lhsT_scale=vs_sg[:, rows],
+                rhs=hid_w[:].bitcast(FP8X4), rhs_scale=hid_s[:], start=True, stop=True,
+            )
+            result = sbuf([P, O], F32, f"result{b}")
+            if b == 0:
+                nc.vector.tensor_copy(result[:], acc[:])
+                nc.sync.dma_start(out[rows, :], result[:])
+            else:
+                nc.scalar.copy(result[:], acc[:])
+                nc.scalar.dma_start(out[rows, :], result[:])

@@ -47,31 +47,42 @@ def tile_picked_tokens_plain_bank_pooledpost_store_plain_kernel(
             for q in quadrants:
                 queue.dma_start(tile[32 * q : 32 * q + 4, :].bitcast(I32), src[0, 4 * q : 4 * q + 4, :].bitcast(I32))
 
+        def load_folded_plane(queue, tile, src):
+            rows = src[0].rearrange("(f q r) n -> q r f n", f=2, q=2)
+            for q in range(2):
+                queue.dma_start(
+                    tile[32 * q : 32 * q + 4, :].rearrange("r (f n) -> r f n", f=2).bitcast(I32), rows[q].bitcast(I32)
+                )
+
+        def unfold_plane(tile):
+            nc.vector.tensor_copy(tile[64:128, :R].bitcast(I32), tile[0:64, R:].bitcast(I32))
+
         def load_words(queue, dtype, width, src, name):
             tile = sbuf([P, width], dtype, name)
             queue.dma_start(tile[:].bitcast(I32), src.bitcast(I32))
             return tile
 
         xo_s = zeroed_plane(M, "xo_s")
+        w2_s = zeroed_plane(2 * R, "w2_s")
+        w_s = zeroed_plane(2 * R, "w_s")
         xt_s = zeroed_plane(T, "xt_s")
-        w2_s = zeroed_plane(R, "w2_s")
-        w_s = zeroed_plane(R, "w_s")
         vs_s = zeroed_plane(V, "vs_s")
         boards = [sbuf([P, C], F32, f"board{t}") for t in range(PACK)]
         for t in range(PACK):
             nc.vector.memset(boards[t][:], 0.0)
 
         l2 = load_list(offs2, "l2")
-        l1 = load_list(offs, "l1")
-        l3 = load_list(offs3, "l3")
-        load_plane(nc.sync, xo_s, xo_scales)
-        xo_w = load_words(nc.sync, U32, M, xo_words[0].rearrange("p n t -> p (n t)"), "xo_w")
+        xo_w = load_words(nc.scalar, U32, M, xo_words[0].rearrange("p n t -> p (n t)"), "xo_w")
+        w_w = load_words(nc.gpsimd, U32, R, w_words[0].rearrange("p n t -> p (n t)"), "w_w")
+        load_plane(nc.scalar, xo_s, xo_scales, range(2))
+        load_plane(nc.sync, xo_s, xo_scales, range(2, 4))
         xt_w = load_words(nc.sync, U16, T, xt_words[0], "xt_w")
-        load_plane(nc.sync, xt_s, xt_scales)
         w2_w = load_words(nc.sync, U16, R, w2_words[0], "w2_w")
-        w_w = load_words(nc.sync, U32, R, w_words[0].rearrange("p n t -> p (n t)"), "w_w")
-        load_plane(nc.sync, w2_s, w2_scales, range(0, 4))
-        load_plane(nc.sync, w_s, w_scales)
+        load_folded_plane(nc.sync, w2_s, w2_scales)
+        load_folded_plane(nc.sync, w_s, w_scales)
+        l1 = load_list(offs, "l1")
+        load_plane(nc.sync, xt_s, xt_scales)
+        l3 = load_list(offs3, "l3")
         sa_t = sbuf([P, PACK], F32, "sa_t")
         nc.sync.dma_start(sa_t[:], sa.rearrange("(p t) o -> p (t o)", t=PACK))
         l4 = load_list(offs4, "l4")
@@ -84,7 +95,14 @@ def tile_picked_tokens_plain_bank_pooledpost_store_plain_kernel(
 
         def deal(copy, src, dtype, name):
             tile = sbuf([P, R], dtype, name)
-            copy(tile[:].rearrange("p (t m) -> p m t", t=PACK), src[:].rearrange("p (m t) -> p m t", t=PACK))
+            copy(tile[:].rearrange("p (t m) -> p m t", t=PACK), src[:, :R].rearrange("p (m t) -> p m t", t=PACK))
+            return tile
+
+        def deal_scales(src, name):
+            tile = sbuf([P, R], U8, name)
+            nc.gpsimd.tensor_copy(
+                tile[:].rearrange("p (t m) -> p t m", t=PACK), src[:, :R].rearrange("p (m t) -> p t m", t=PACK)
+            )
             return tile
 
         def gather(src, offsets, count, dtype, name):
@@ -97,13 +115,15 @@ def tile_picked_tokens_plain_bank_pooledpost_store_plain_kernel(
 
         xo_sg = gather(xo_s, l2[:], J, U8, "xo_sg")
         xo_wg = gather(xo_w, l2[:], J, U32, "xo_wg")
-        w2_sd = deal(nc.vector.tensor_copy, w2_s, U8, "w2_sd")
-        w_sd = deal(nc.vector.tensor_copy, w_s, U8, "w_sd")
+        unfold_plane(w2_s)
+        unfold_plane(w_s)
+        w2_sd = deal_scales(w2_s, "w2_sd")
+        w_sd = deal_scales(w_s, "w_sd")
         halves = [l1[:, h * HALF // 16 : (h + 1) * HALF // 16] for h in range(2)]
         xt_wg = [gather(xt_w, halves[0], HALF, U16, "xt_wg0")]
         xt_sg = [gather(xt_s, halves[0], HALF, U8, "xt_sg0")]
-        xt_wg.append(gather(xt_w, halves[1], HALF, U16, "w2_s"))
-        xt_sg.append(gather(xt_s, halves[1], HALF, U8, "w_s"))
+        xt_wg.append(gather(xt_w, halves[1], HALF, U16, "xt_wg1"))
+        xt_sg.append(gather(xt_s, halves[1], HALF, U8, "xt_sg1"))
 
         def product(acc, t, h, notes_first):
             rows = slice(t * P, (t + 1) * P)
@@ -123,21 +143,20 @@ def tile_picked_tokens_plain_bank_pooledpost_store_plain_kernel(
         a, picks, pooled = {}, {}, {}
         woven = sbuf([P, O, PACK], BF16, "woven")
 
+        for h, copy in enumerate((nc.scalar.copy, nc.vector.tensor_copy)):
+            for t in range(2):
+                if h == 0:
+                    a[t] = sbuf([P, J], F32, f"a{t}")
+                bank = psum.tile([P, HALF], F32, name=f"half{t}{h}")
+                product(bank[:], t, h, True)
+                copy(a[t][:, h * HALF : (h + 1) * HALF], bank[:])
+
         def finish_a(t):
-            if t < 2:
-                a[t] = sbuf([P, J], F32, f"a{t}")
-                first = psum.tile([P, HALF], F32, name=f"first{t}")
-                second = psum.tile([P, HALF], F32, name=f"second{t}")
-                product(first[:], t, 0, True)
-                product(second[:], t, 1, True)
-                nc.scalar.copy(a[t][:, :HALF], first[:])
-                nc.vector.tensor_copy(a[t][:, HALF:], second[:])
-            else:
-                a[t] = sbuf([P, J], F32, f"picks{t - 2}")
-                both = psum.tile([P, J], F32, name=f"both{t}")
-                product(both[:, HALF:], t, 1, False)
-                product(both[:, :HALF], t, 0, False)
-                nc.vector.tensor_copy(a[t][:], both[:])
+            a[t] = sbuf([P, J], F32, f"picks{t - 2}")
+            both = psum.tile([P, J], F32, name=f"both{t}")
+            product(both[:, HALF:], t, 1, False)
+            product(both[:, :HALF], t, 0, False)
+            nc.vector.tensor_copy(a[t][:], both[:])
 
         def pick(t):
             picks[t] = sbuf([P, S], F32, f"picks{t}")
@@ -150,8 +169,6 @@ def tile_picked_tokens_plain_bank_pooledpost_store_plain_kernel(
         def put(t):
             nc.scalar.activation(boards[t][:].indirect(l4[:]), pooled[t][:], COPY)
 
-        finish_a(0)
-        finish_a(1)
         pick(0)
         for t in range(PACK):
             pool_pairs(t)

from contextlib import ExitStack

import concourse.mybir as mybir

F32 = mybir.dt.float32
BF16 = mybir.dt.bfloat16
I32 = mybir.dt.int32
U32 = mybir.dt.uint32
U16 = mybir.dt.uint16
U8 = mybir.dt.uint8
FP8X4 = mybir.dt.float8_e4m3fn_x4
FP4X4 = mybir.dt.float4_e2m1fn_x4
COPY = mybir.ActivationFunctionType.Copy
MAX = mybir.AluOpType.max

K, J, R, T, Z, M, S, U, C, O, N, V = 512, 512, 512, 2048, 512, 1024, 256, 128, 256, 128, 256, 1024
FLOPS = 2 * K * R * J + 2 * Z * R * J + 2 * R * N * O

P = 128
PACK = 4
HALF = J // 2


def tile_picked_tokens_plain_bank_pooledpost_store_plain_kernel(
    tc, xt_words, xt_scales, w_words, w_scales, xo_words, xo_scales, w2_words, w2_scales,
    sa, sb, vs_words, vs_scales, offs, offs2, offs3, offs4, offs5, offs6, out,
):
    nc = tc.nc
    with ExitStack() as ctx:
        keep = ctx.enter_context(tc.tile_pool(name="keep", bufs=1))
        psum = ctx.enter_context(tc.psum_pool(name="psum", bufs=1))

        def sbuf(shape, dtype, name):
            return keep.tile(shape, dtype, name=name, align_bytes=64)

        def load_list(src, name):
            tile = keep.tile(list(src.shape), U16, name=name)
            nc.sync.dma_start(tile[:], src)
            return tile

        def zeroed_plane(width, name):
            tile = sbuf([P, width], U8, name)
            nc.vector.memset(tile[:].bitcast(I32), 0)
            return tile

        def load_plane(queue, tile, src, quadrants=range(4)):
            for q in quadrants:
                queue.dma_start(tile[32 * q : 32 * q + 4, :].bitcast(I32), src[0, 4 * q : 4 * q + 4, :].bitcast(I32))

        def load_folded_plane(queue, tile, src):
            rows = src[0].rearrange("(f q r) n -> q r f n", f=2, q=2)
            for q in range(2):
                queue.dma_start(
                    tile[32 * q : 32 * q + 4, :].rearrange("r (f n) -> r f n", f=2).bitcast(I32), rows[q].bitcast(I32)
                )

        def unfold_plane(tile):
            nc.vector.tensor_copy(tile[64:128, :R].bitcast(I32), tile[0:64, R:].bitcast(I32))

        def load_words(queue, dtype, width, src, name):
            tile = sbuf([P, width], dtype, name)
            queue.dma_start(tile[:].bitcast(I32), src.bitcast(I32))
            return tile

        xo_s = zeroed_plane(M, "xo_s")
        w2_s = zeroed_plane(2 * R, "w2_s")
        w_s = zeroed_plane(2 * R, "w_s")
        xt_s = zeroed_plane(T, "xt_s")
        vs_s = zeroed_plane(V, "vs_s")
        boards = [sbuf([P, C], F32, f"board{t}") for t in range(PACK)]
        for t in range(PACK):
            nc.vector.memset(boards[t][:], 0.0)

        l2 = load_list(offs2, "l2")
        xo_w = load_words(nc.scalar, U32, M, xo_words[0].rearrange("p n t -> p (n t)"), "xo_w")
        w_w = load_words(nc.gpsimd, U32, R, w_words[0].rearrange("p n t -> p (n t)"), "w_w")
        load_plane(nc.scalar, xo_s, xo_scales, range(2))
        load_plane(nc.sync, xo_s, xo_scales, range(2, 4))
        xt_w = load_words(nc.sync, U16, T, xt_words[0], "xt_w")
        w2_w = load_words(nc.sync, U16, R, w2_words[0], "w2_w")
        load_folded_plane(nc.sync, w2_s, w2_scales)
        load_folded_plane(nc.sync, w_s, w_scales)
        l1 = load_list(offs, "l1")
        load_plane(nc.sync, xt_s, xt_scales)
        l3 = load_list(offs3, "l3")
        sa_t = sbuf([P, PACK], F32, "sa_t")
        nc.sync.dma_start(sa_t[:], sa.rearrange("(p t) o -> p (t o)", t=PACK))
        l4 = load_list(offs4, "l4")
        l5 = load_list(offs5, "l5")
        sb_t = sbuf([P, PACK], F32, "sb_t")
        nc.sync.dma_start(sb_t[:], sb.rearrange("(p t) o -> p (t o)", t=PACK))
        l6 = load_list(offs6, "l6")
        vs_w = load_words(nc.sync, U16, V, vs_words[0], "vs_w")
        load_plane(nc.sync, vs_s, vs_scales)

        def deal(copy, src, dtype, name):
            tile = sbuf([P, R], dtype, name)
            copy(tile[:].rearrange("p (t m) -> p m t", t=PACK), src[:, :R].rearrange("p (m t) -> p m t", t=PACK))
            return tile

        def deal_scales(src, name):
            tile = sbuf([P, R], U8, name)
            nc.gpsimd.tensor_copy(
                tile[:].rearrange("p (t m) -> p t m", t=PACK), src[:, :R].rearrange("p (m t) -> p t m", t=PACK)
            )
            return tile

        def gather(src, offsets, count, dtype, name):
            tile = sbuf([P, count], dtype, name)
            nc.vector.tensor_copy(tile[:], src[:].indirect(offsets))
            return tile

        w2_wd = deal(nc.scalar.copy, w2_w, U16, "w2_wd")
        w_wd = deal(nc.scalar.copy, w_w, U32, "w_wd")

        xo_sg = gather(xo_s, l2[:], J, U8, "xo_sg")
        xo_wg = gather(xo_w, l2[:], J, U32, "xo_wg")
        unfold_plane(w2_s)
        unfold_plane(w_s)
        w2_sd = deal_scales(w2_s, "w2_sd")
        w_sd = deal_scales(w_s, "w_sd")
        halves = [l1[:, h * HALF // 16 : (h + 1) * HALF // 16] for h in range(2)]
        xt_wg = [gather(xt_w, halves[0], HALF, U16, "xt_wg0")]
        xt_sg = [gather(xt_s, halves[0], HALF, U8, "xt_sg0")]
        xt_wg.append(gather(xt_w, halves[1], HALF, U16, "xt_wg1"))
        xt_sg.append(gather(xt_s, halves[1], HALF, U8, "xt_sg1"))

        def product(acc, t, h, notes_first):
            rows = slice(t * P, (t + 1) * P)
            cols = slice(h * HALF, (h + 1) * HALF)
            notes = dict(
                lhsT=w2_wd[:, rows].bitcast(FP4X4), lhsT_scale=w2_sd[:, rows],
                rhs=xo_wg[:, cols].bitcast(FP8X4), rhs_scale=xo_sg[:, cols],
            )
            tokens = dict(
                lhsT=w_wd[:, rows].bitcast(FP8X4), lhsT_scale=w_sd[:, rows],
                rhs=xt_wg[h][:].bitcast(FP4X4), rhs_scale=xt_sg[h][:],
            )
            opening, closing = (notes, tokens) if notes_first else (tokens, notes)
            nc.tensor.matmul_mx(acc, start=True, stop=False, **opening)
            nc.tensor.matmul_mx(acc, start=False, stop=True, **closing)

        a, picks, pooled = {}, {}, {}
        woven = sbuf([P, O, PACK], BF16, "woven")

        for h, copy in enumerate((nc.scalar.copy, nc.vector.tensor_copy)):
            for t in range(2):
                if h == 0:
                    a[t] = sbuf([P, J], F32, f"a{t}")
                bank = psum.tile([P, HALF], F32, name=f"half{t}{h}")
                product(bank[:], t, h, True)
                copy(a[t][:, h * HALF : (h + 1) * HALF], bank[:])

        def finish_a(t):
            a[t] = sbuf([P, J], F32, f"picks{t - 2}")
            both = psum.tile([P, J], F32, name=f"both{t}")
            product(both[:, HALF:], t, 1, False)
            product(both[:, :HALF], t, 0, False)
            nc.vector.tensor_copy(a[t][:], both[:])

        def pick(t):
            picks[t] = sbuf([P, S], F32, f"picks{t}")
            nc.scalar.activation(picks[t][:], a[t][:].indirect(l3[:]), COPY, scale=sa_t[:, t : t + 1])

        def pool_pairs(t):
            pooled[t] = sbuf([P, U], F32, f"pooled{t}")
            nc.vector.tensor_tensor(pooled[t][:], picks[t][:, 0:S:2], picks[t][:, 1:S:2], MAX)

        def put(t):
            nc.scalar.activation(boards[t][:].indirect(l4[:]), pooled[t][:], COPY)

        pick(0)
        for t in range(PACK):
            pool_pairs(t)
            if t + 2 < PACK:
                finish_a(t + 2)
            if t + 1 < PACK:
                pick(t + 1)
            put(t)

        vs_sg = gather(vs_s, l6[:], N, U8, "picks2")
        vs_wg = gather(vs_w, l6[:], N, U16, "picks1")

        hid = sbuf([P, PACK, O], BF16, "picks3")
        for t in range(PACK):
            nc.scalar.activation(hid[:, t, :], boards[t][:].indirect(l5[:]), COPY, scale=sb_t[:, t : t + 1])
        nc.vector.tensor_copy(woven[:, :, 0:2], hid[:, 0:2, :].rearrange("p t o -> p o t"))
        nc.vector.tensor_copy(woven[:, :, 2], hid[:, 2, :])
        nc.vector.tensor_copy(woven[:, :, 3], hid[:, 3, :])
        hid_w = sbuf([P, O], U32, "hid_w")
        hid_s = sbuf([P, O], U8, "hid_s")
        nc.vector.quantize_mx(out=hid_w[:].bitcast(FP8X4), scales=hid_s[:], in_=woven[:].rearrange("p o t -> p (o t)"))

        for b in range(N // P):
            rows = slice(b * P, (b + 1) * P)
            acc = psum.tile([P, O], F32, name=f"acc{b}")
            nc.tensor.matmul_mx(
                acc[:], lhsT=vs_wg[:, rows].bitcast(FP4X4), lhsT_scale=vs_sg[:, rows],
                rhs=hid_w[:].bitcast(FP8X4), rhs_scale=hid_s[:], start=True, stop=True,
            )
            result = sbuf([P, O], F32, f"result{b}")
            if b == 0:
                nc.vector.tensor_copy(result[:], acc[:])
                nc.sync.dma_start(out[rows, :], result[:])
            else:
                nc.scalar.copy(result[:], acc[:])
                nc.scalar.dma_start(out[rows, :], result[:])
